import numpy as np, ml_dtypes
CORES = [3,11,19,27,35,43,51,59]
N = 8
import mx_ref
BF = ml_dtypes.bfloat16
def entries(a):
    return np.ascontiguousarray(a.T).reshape(-1)
def table(e):
    return np.ascontiguousarray(np.reshape(e, (-1, 16)).T).astype(np.int32)
def pick(q, e):
    c = np.concatenate([q[0].reshape(128, -1, 4), np.zeros((128, 1, 4), np.uint8)], axis=1); s = np.concatenate([q[1], np.ones((16, 1), np.uint8)], axis=1)
    return (np.ascontiguousarray(c[:, e].reshape(128, -1)), np.ascontiguousarray(s[:, e]))
def join(*qs):
    return (np.concatenate([q[0] for q in qs], axis=1), np.concatenate([q[1] for q in qs], axis=1))
def put(q, e, v):
    c, s = q[0].reshape(128, -1, 4).copy(), q[1].copy(); c[:, e] = v[0].reshape(128, -1, 4); s[:, e] = v[1]
    return (c.reshape(128, -1), s)
def pk(c, s):
    return (np.ascontiguousarray(c), mx_ref.live(s))
def emit(q):
    return q[0], q[1]
def packed(v, rng):
    q = [mx_ref.quantize(np.ascontiguousarray(v[r])) for r in range(N)]
    return np.stack([a for a, b in q]), np.stack([mx_ref.plane(b, rng) for a, b in q])
def decode(q):
    o = []
    for b in range(4):
        e = np.zeros((128, 128, 4), np.float32); e[np.arange(128), np.arange(128), b] = 1
        o.append(mx_ref.matmul(mx_ref.quantize(e.reshape(128, 512).astype(BF)), q))
    return np.stack(o, axis=2).reshape(128, -1)
def f(rng, *shape):
    return mx_ref.flush((rng.standard_normal(shape, dtype=np.float32) * np.exp2(rng.integers(-2, 3, shape[:-1] + (1,)))).astype(BF))
def wide(rng, *shape, cols=0):
    v = rng.standard_normal(shape, dtype=np.float32) * np.exp2(rng.integers(-12, 13, shape)).astype(np.float32)
    if cols: v *= np.repeat(np.exp2(rng.integers(-cols, cols + 1, shape[:-2] + (1, shape[-1] // 4))) * (rng.random(shape[:-2] + (1, shape[-1] // 4)) > 0.0625), 4, axis=-1).astype(np.float32)
    return mx_ref.flush(v.astype(BF))
C, S, CAPP = 1024, 256, 48
def big(v, k):
    v = v.astype(np.float32) * np.float32(k)
    v[np.abs(v) < np.float32(2.0 ** -16)] = 0
    return v.astype(BF)
def names(rng, n, each):
    out, at, m = [None] * N, 0, int(n.sum())
    if not each:
        left = np.full(C, 2)
        for s in rng.permutation(N):
            out[s] = rng.permutation(np.flatnonzero(left))[:n[s]]; left[out[s]] -= 1
        return out
    a = rng.permutation(C)[:m // each]
    if each == 2: a = np.concatenate([a, rng.permutation(a)])
    for s in rng.permutation(N):
        out[s] = a[at:at + n[s]]; at += n[s]
    return out
def lists(rng, each=0, full=False, gaps=False, silent=False):
    sn, tc = np.full((N, N * CAPP), -1), np.full((N, N * CAPP), -1)
    n = np.full((N, N), CAPP) if full else rng.integers(CAPP // 4, CAPP, (N, N))
    if gaps: n[:] = CAPP - CAPP // 6
    if silent: n[:, int(rng.integers(0, N))] = 0
    for q in range(N):
        t = names(rng, n[:, q], each)
        for s in range(N): tc[q, s * CAPP + rng.permutation(CAPP)[:n[s, q]]] = t[s]
    for s in range(N):
        used = np.concatenate([tc[q, s * CAPP:s * CAPP + CAPP] >= 0 for q in range(N)])
        e = np.concatenate([rng.permutation(S), rng.integers(0, S, N * CAPP)])[:used.sum()]
        sn[s, used] = rng.permutation(e)
    return {"sn": np.stack([table(v) for v in sn]), "tc": np.stack([table(v) for v in tc])}
def setup_inputs(rng):
    c, p = packed(big(f(rng, N, 128, 4 * C), 1), rng)
    return {"wc": c, "ws": p, "gr": big(f(rng, N, 128, 4 * S), 8), **lists(rng)}
def setup_inputs_cancel(rng):
    tc, P = lists(rng, each=2, full=True, gaps=True)["tc"], S // 2
    x = rng.integers(4, 8, (128, P, 4)) * np.exp2(rng.integers(-2, 1, (128, P, 4))) * rng.choice([-1.0, 1.0], (128, P, 4)) * np.exp2(rng.integers(-2, 3, (128, P, 1)))
    h = rng.integers(0, P, (N, C))
    c, p = packed(np.stack([x[:, h[q]].reshape(128, -1) for q in range(N)]).astype(np.float32).astype(BF), rng)
    g, sn = np.zeros((N, 128, S, 4), np.float32), np.full((N, N * CAPP), -1)
    at = np.stack([rng.permutation(S) for s in range(N)])
    for s in range(N):
        g[s][:, at[s, :P]] = 8 * x
        g[s][:, at[s, P:]] = 8 * x * np.exp2(-rng.integers(21, 25, (P, 1)))
    for q in range(N):
        t = entries(tc[q]).reshape(N, CAPP)
        o = rng.permutation(np.unique(t[t >= 0]))
        late, seen = np.zeros(C, bool), np.zeros(C, bool)
        late[o[:o.size // 2]] = True
        for s in range(N):
            k = np.flatnonzero(t[s] >= 0); e = t[s][k]
            small = seen[e] != late[e]
            sn[s, q * CAPP + k] = at[s][P * small + h[q, e]]
            seen[e] = True
    return {"wc": c, "ws": p, "gr": g.reshape(N, 128, 4 * S).astype(BF), "sn": np.stack([table(v) for v in sn]), "tc": tc}
def setup_inputs_full(rng):
    return {**setup_inputs(rng), **lists(rng, full=True)}
def setup_inputs_most(rng):
    return {**setup_inputs(rng), **lists(rng, each=1, full=True, silent=True)}
def setup_inputs_spread(rng):
    d = setup_inputs(rng)
    d["wc"], d["ws"] = packed(big(wide(rng, N, 128, 4 * C, cols=8), 1), rng)
    d["gr"] = big(wide(rng, N, 128, 4 * S, cols=8), 8)
    return d
def setup_inputs_twice(rng):
    return {**setup_inputs(rng), **lists(rng, each=2, full=True)}
def check_inputs(d):
    b = []
    for r in range(N):
        a, t = entries(d["sn"][r]), entries(d["tc"][r])
        if a.min() < -1 or a.max() >= S: b.append("sn")
        sent = np.concatenate([entries(d["sn"][s])[r * CAPP:r * CAPP + CAPP] for s in range(N)])
        bad = t.min() < -1 or t.max() >= C or ((t >= 0) != (sent >= 0)).any()
        for s in range(N):
            v = t[s * CAPP:s * CAPP + CAPP]; v = v[v >= 0]
            bad = bad or len(set(v.tolist())) != v.size
        if bad or (np.unique(t[t >= 0], return_counts=True)[1] > 2).any(): b.append("tc")
    return b
def reference(wc, ws, gr, sn, tc):
    oc, osc, up = np.zeros((N, 128, 4 * C), np.uint8), np.zeros((N, 16, C), np.uint8), np.zeros((N, 1, C), np.float32)
    g = [decode(mx_ref.quantize(np.ascontiguousarray(gr[s]))).reshape(128, S, 4) for s in range(N)]
    for q in range(N):
        w = pk(wc[q], ws[q])
        v = decode(w).reshape(128, C, 4)
        for s in range(N):
            e, t = entries(sn[s])[q * CAPP:q * CAPP + CAPP], entries(tc[q])[s * CAPP:s * CAPP + CAPP]
            k = t >= 0
            v[:, t[k]] = v[:, t[k]] - g[s][:, e[k]] * np.float32(0.125)
            up[q, 0, t[k]] += 1
        named = np.flatnonzero(up[q, 0])
        new = mx_ref.quantize(np.ascontiguousarray(v.reshape(128, -1).astype(BF)))
        oc[q], osc[q] = emit(put(w, named, pick(new, named)))
    return {"oc": oc, "osc": osc, "up": up}

@@ -1,0 +1,426 @@
+from concourse.bass import DstId, RemoteDMATransfer
+from concourse.mybir import dt, AluOpType as Op, ActivationFunctionType as Fn
+
+C, S, CAP, N = 1024, 256, 48, 8
+KEY = 2048
+NONE = N * KEY
+NEW = 1024
+ZERO = 128
+NA, NB, B0 = 240, 144, 256
+ALL = B0 + NB
+
+E4, U8, F32, I32, U16, BF = "float8_e4m3fn_x4", "uint8", "float32", "int32", "uint16", "bfloat16"
+
+
+def _sb(n, d):
+    return ("sbuf", [128, n], d)
+
+
+SCRATCH = {
+    "grt": _sb(4 * S, BF), "gq": _sb(S, E4), "gs": _sb(S, U8),
+    "snw": _sb(24, I32), "soff": _sb(26, U16),
+    "slotq": _sb(336, E4), "slots": _sb(336, U8),
+    "landq": _sb(ZERO + ALL, E4), "lands": _sb(ZERO + ALL, U8),
+    "zt": _sb(512, BF), "eo": _sb(516, BF), "ef": _sb(516, BF), "en": _sb(516, BF),
+    "eq": _sb(1024, E4), "es": _sb(1024, U8),
+    "wq": _sb(C, E4), "wqs": _sb(C, U8),
+    "finq": _sb(NEW + ZERO + ALL, E4), "fins": _sb(NEW + ZERO + ALL, U8),
+    "wselq": _sb(ALL, E4), "wsels": _sb(ALL, U8),
+    "firq": _sb(ALL, E4), "firs": _sb(ALL, U8),
+    "secq": _sb(ALL, E4), "secs": _sb(ALL, U8),
+    "h": _sb(4 * ALL, BF),
+    "outq": _sb(C, E4), "outs": _sb(C, U8),
+    "tcw": _sb(24, I32), "ta": _sb(24, I32), "tb": _sb(24, I32), "tx": _sb(24, I32), "ty": _sb(24, I32),
+    "tz": _sb(24, I32),
+    "off4": _sb(32, U16), "wl": _sb(26, U16), "fsl": _sb(52, U16), "finl": _sb(64, U16), "upl": _sb(64, U16),
+    "pidx": _sb(2, I32), "pa": _sb(2, I32), "pcol": _sb(4, F32),
+    "m16": _sb(16, I32), "m16a": _sb(16, I32), "mk": _sb(ALL, F32), "seg": _sb(ALL, F32),
+    "vb": _sb(26, F32), "vw": _sb(26, F32), "cb": _sb(24, F32), "cl": _sb(24, F32),
+    "b48": _sb(48, F32), "vr": _sb(ALL, F32), "tab": _sb(C + CAP, F32), "pv": _sb(ALL, F32),
+    "sc1": _sb(ALL, F32), "sc2": _sb(ALL, F32), "fs": _sb(52, I32), "fa": _sb(52, I32),
+    "tw": _sb(64, F32), "ti": _sb(64, I32), "tf": _sb(64, I32),
+    "hup": _sb(16 + ALL, F32), "upr": _sb(C, F32),
+    "psa": ("psum", [128, 2048], F32), "psb": ("psum", [128, 2048], F32),
+}
+SEMAPHORES = ["vec", "act", "ten", "gpc", "dsn", "dgr", "dtc", "dwc", "dws", "dfq", "dfs", "dwrap", "dout",
+              "arrec", "arres", "arrlc", "arrls", "sent", "issued"]
+
+
+def _pairs(T, topo):
+    out = []
+    for r in range(N):
+        if not any(r in p for p in out):
+            out.append([x for x in range(N)
+                        if x == r or topo.mates(topo.chip(T.cores[r]), topo.chip(T.cores[x]))])
+    return out
+
+
+def _stages(s, pairs):
+    u = [i for i, p in enumerate(pairs) if s in p][0]
+    n = len(pairs)
+    one = sorted(pairs[(u + 1) % n] + pairs[(u + 2) % n])
+    two = sorted(pairs[(u + 3) % n] + [x for x in pairs[u] if x != s])
+    return one, two
+
+
+def _engines(s, stage, T, topo):
+    src = T.cores[s]
+    have = len(topo.engines(src, T.cores[stage[0]]))
+    size = 1
+    while 2 * size * len(stage) <= have:
+        size *= 2
+    spare = have - size * len(stage)
+    out, at = {}, 0
+    for q in stage:
+        a, b = topo.chip(src), topo.chip(T.cores[q])
+        n = size
+        if spare >= size and not topo.mates(a, b) and not topo.same_plane(a, b):
+            n, spare = 2 * size, spare - size
+        out[q] = topo.engines(src, T.cores[q])[at:at + n]
+        at += n
+    return out
+
+
+def _chain(q, pairs):
+    early = [s for s in range(N) if s != q and q in _stages(s, pairs)[0]]
+    late = [s for s in range(N) if s != q and q in _stages(s, pairs)[1]]
+    return [q] + early + late
+
+
+def _pos(t):
+    return CAP * t if t < NA // CAP else CAP * t + B0 - NA
+
+
+def _runs(ranks):
+    out = []
+    for i, r in enumerate(ranks):
+        if out and out[-1][1] + out[-1][2] == r:
+            out[-1][2] += 1
+        else:
+            out.append([i, r, 1])
+    return out
+
+
+def rank_program(g, core, T, topo):
+    me = T.rank_of(core)
+    if me is None:
+        return
+    sem = T.sem
+    ve, sc, te, sy = g.vector, g.scalar, g.tensor, g.sync
+    cnt, seen = {}, {}
+
+    def inc(name, ins, by=1):
+        ins.then_inc(sem[name], by)
+        cnt[name] = cnt.get(name, 0) + by
+        return cnt[name]
+
+    def V(ins):
+        return inc("vec", ins)
+
+    def A(ins):
+        return inc("act", ins)
+
+    def G(ins):
+        return inc("gpc", ins)
+
+    def wait(qn, name, val):
+        if seen.get((qn, name), 0) < val:
+            seen[(qn, name)] = val
+            {"v": ve, "s": sc, "t": te, "y": sy, "g": g}[qn].wait_ge(sem[name], val)
+
+    pairs = _pairs(T, topo)
+    one, two = _stages(me, pairs)
+    chain = _chain(me, pairs)
+    u8, u32 = dt.uint8, dt.uint32
+
+    inc("dgr", sy.dma_start(T.grt[:], T.gr[:]), 16)
+    for k in range(8):
+        inc("dsn", (sc if k < 5 else sy).dma_start(T.snw[16 * k:16 * k + 16, :], T.sn[:]), 16)
+    for k in range(8):
+        inc("dtc", (sc if k < 3 else sy).dma_start(T.tcw[16 * k:16 * k + 16, :], T.tc[:]), 16)
+    inc("dwc", sy.dma_start(T.wq[:].bitcast(u8), T.wc[:]), 16)
+    inc("dws", sc.dma_start(T.wqs[:], T.ws[:]), 16)
+
+    v_eo = V(ve.memset(T.eo[:], 1.0))
+    v_zt = V(ve.memset(T.zt[:], 0.0))
+    p_tab = G(g.iota(T.tab[:, 0:64], [[16, 64]], NONE, 0, allow_small_or_imprecise_dtypes=True))
+    p_b48 = G(g.iota(T.b48[:], [[1, 48]], 0, 0, allow_small_or_imprecise_dtypes=True))
+    p_m16 = G(g.iota(T.m16[:], [[1, 16]], 128, -1))
+    p_idx = G(g.iota(T.pidx[:], [[0, 2]], 0, 1))
+    p_cb = G(g.iota(T.cb[:], [[0, 8], [16, 3]], C, 0, allow_small_or_imprecise_dtypes=True))
+    p_vb = G(g.iota(T.vb[:, 0:25], [[16, 25]], NEW + ZERO, 0, allow_small_or_imprecise_dtypes=True))
+    wait("g", "vec", v_eo)
+    p_ef = G(g.affine_select(T.ef[:], T.eo[:], [[1, 516]], Op.is_equal, 0.0, -3, -4))
+
+    wait("s", "gpc", p_tab)
+    a_tab = 0
+    for r in (1, 2, 4, 8):
+        if a_tab:
+            wait("s", "act", a_tab)
+        a_tab = A(sc.activation(T.tab[:, 64 * r:128 * r], T.tab[:, 0:64 * r], Fn.Identity, bias=float(r)))
+    wait("s", "gpc", p_b48)
+    for t, s in enumerate(chain):
+        x = _pos(t)
+        a_vr = A(sc.activation(T.vr[:, x:x + CAP], T.b48[:], Fn.Identity, bias=float(KEY * s + NEW + ZERO + x)))
+
+    V(ve.memset(T.pv[:, 0:CAP], float(NONE)))
+    V(ve.memset(T.pv[:, NA:B0], float(NONE)))
+    V(ve.memset(T.tab[:, C:C + CAP], float(NONE)))
+    V(ve.memset(T.fs[:], 0))
+    V(ve.memset(T.wl[:], 0))
+    wait("v", "vec", v_zt)
+    v_zq = V(ve.quantize_mx(T.landq[:, 0:ZERO], T.lands[:, 0:ZERO], T.zt[:]))
+    wait("v", "gpc", p_m16)
+    v = V(ve.tensor_scalar(T.m16a[:], T.m16[:], 15, None, Op.bitwise_and))
+    wait("v", "gpc", p_idx)
+    v_pa = V(ve.tensor_scalar(T.pa[:], T.pidx[:], 15, None, Op.bitwise_and))
+    wait("v", "vec", v)
+    v_mk = V(ve.tensor_scalar(T.mk[:, 0:16], T.m16a[:], 0.0, None, Op.is_equal))
+    wait("v", "vec", v_pa)
+    v_pc = V(ve.tensor_copy(T.pcol[:, 0:1], T.pa[:, 0:1]))
+    wait("v", "gpc", p_cb)
+    wait("v", "vec", v_pc)
+    V(ve.tensor_scalar(T.cl[:], T.cb[:], T.pcol[:, 0:1], None, Op.add))
+
+    wait("s", "vec", v_mk)
+    a_mk, n = 0, 16
+    while n < ALL:
+        m = min(n, ALL - n)
+        if a_mk:
+            wait("s", "act", a_mk)
+        a_mk = A(sc.activation(T.mk[:, n:n + m], T.mk[:, 0:m], Fn.Copy))
+        n += m
+
+    def unit(k, src):
+        b = k % 4
+        return V(ve.quantize_mx(T.eq[:, 128 * k:128 * k + 128], T.es[:, 128 * k:128 * k + 128],
+                                src[:, 3 - b:3 - b + 512]))
+
+    wait("v", "gpc", p_ef)
+    for k in range(4):
+        v_ep = unit(k, T.ef)
+
+    wait("v", "dsn", cnt["dsn"])
+    for base, ranks in ((0, one), (12, two), (22, [me])):
+        for i, r, n in _runs(ranks):
+            V(ve.tensor_copy(T.soff[:, base + 3 * i:base + 3 * (i + n)], T.snw[:, 3 * r:3 * (r + n)]))
+    wait("v", "dgr", cnt["dgr"])
+    v_gq = V(ve.quantize_mx(T.gq[:], T.gs[:], T.grt[:]))
+
+    def pickc(out, a, b, win, w0, w1, off, o0, o1):
+        return V(ve.tensor_copy(out[:, a:b].bitcast(u32), win[:, w0:w1].bitcast(u32).indirect(off[:, o0:o1])))
+
+    def picks(out, a, b, win, w0, w1, off, o0, o1):
+        return A(sc.activation(out[:, a:b], win[:, w0:w1].indirect(off[:, o0:o1]), Fn.Copy))
+
+    wait("v", "vec", v_gq)
+    wait("s", "vec", v_gq)
+    n1, n2 = CAP * len(one), CAP * (len(one) + len(two))
+    sends = []
+    for stage, a, b, o0, o1, cs, ss in ((one, 0, n1, 0, 12, "arrec", "arres"), (two, n1, n2, 12, 21, "arrlc", "arrls")):
+        vp = pickc(T.slotq, a, b, T.gq, 0, S, T.soff, o0, o1)
+        ap = picks(T.slots, a, b, T.gs, 0, S, T.soff, o0, o1)
+        sends.append((stage, a, vp, ap, cs, ss))
+    sent = 0
+    for stage, a, vp, ap, cs, ss in sends:
+        eng = _engines(me, stage, T, topo)
+        for codes in (True, False):
+            wait("g", "vec" if codes else "act", vp if codes else ap)
+            tr = []
+            for i, q in enumerate(stage):
+                rid, pid, _se = topo.addr(T.cores[q])
+                x = a + CAP * i
+                y = ZERO + _pos(_chain(q, pairs).index(me))
+                src, dst = ((T.slotq[:, x:x + CAP].bitcast(u8), T.landq[:, y:y + CAP].bitcast(u8)) if codes
+                            else (T.slots[:, x:x + CAP], T.lands[:, y:y + CAP]))
+                tr.append(RemoteDMATransfer(dst_ids=[DstId(rid=rid, pnc=pid)],
+                                            dma_engine_mask=sum(1 << e for e in eng[q]),
+                                            remote_sem=sem[cs if codes else ss], src=src, dst=dst))
+                sent += len(eng[q])
+            g.remote_dma_fused(tr, local_sem=sem["sent"])
+    g.sem_inc(sem["issued"], 1)
+
+    wait("y", "issued", 1)
+    inc("dfq", sy.dma_start(T.finq[:, 0:C].bitcast(u8), T.wc[:]), 16)
+    inc("dfs", sy.dma_start(T.fins[:, 0:C], T.ws[:]), 16)
+
+    v_own = pickc(T.landq, ZERO, ZERO + CAP, T.gq, 0, S, T.soff, 22, 25)
+    a_own = picks(T.lands, ZERO, ZERO + CAP, T.gs, 0, S, T.soff, 22, 25)
+
+    wait("v", "dtc", cnt["dtc"])
+    v1 = V(ve.tensor_scalar(T.ta[:], T.tcw[:], 15, None, Op.bitwise_and))
+    V(ve.tensor_scalar(T.tb[:], T.tcw[:], 2047, 4, Op.bitwise_and, Op.logical_shift_right))
+    wait("v", "vec", v1)
+    v1 = V(ve.tensor_scalar(T.tx[:], T.ta[:], 64.0, None, Op.mult))
+    wait("v", "vec", v1)
+    v1 = V(ve.tensor_tensor(T.ty[:], T.tx[:], T.tb[:], Op.add))
+    wait("v", "vec", v1)
+    v1 = V(ve.tensor_tensor(T.tz[:], T.ty[:], T.cl[:], Op.min))
+    wait("v", "vec", v1)
+    for i in range(3):
+        v_off = V(ve.tensor_copy(T.off4[:, i:32:4], T.tz[:, i:24:3]))
+
+    late, todo = {}, []
+
+    def do_wl(a, b, x, y):
+        late["wl"] = V(ve.tensor_copy(T.wl[:, a:b], T.tcw[:, x:y]))
+
+    def do_vw(c, n, key):
+        wait("v", "gpc", p_vb)
+        late["vw"] = V(ve.tensor_scalar(T.vw[:, c:c + n], T.vb[:, c:c + n], T.pcol[:, 0:1], float(key), Op.add, Op.add))
+
+    def do_seg(start):
+        if start:
+            late["seg"] = V(ve.memset(T.seg[:], 1.0))
+        else:
+            wait("v", "vec", late["seg"])
+            V(ve.memset(T.seg[:, 0:ALL:16], 0.0))
+
+    def do_en():
+        late["en"] = V(ve.tensor_scalar(T.en[:], T.ef[:], -0.125, None, Op.mult))
+
+    def do_em(k):
+        wait("v", "vec", late["en"])
+        late["em"] = unit(k, T.en)
+
+    for base, ranks in ((0, chain[:5]), (16, chain[5:])):
+        for i, r, n in _runs(ranks):
+            todo.append((do_wl, (base + 3 * i, base + 3 * (i + n), 3 * r, 3 * (r + n))))
+    todo.append((do_seg, (True,)))
+    for k, s in enumerate(chain):
+        todo.append((do_vw, (_pos(k) // 16, 3, KEY * s)))
+    todo.append((do_vw, (15, 1, 0)))
+    todo.append((do_seg, (False,)))
+    todo.append((do_en, ()))
+    todo.append((lambda: V(ve.memset(T.hup[:, 0:16], -3.0)), ()))
+    for k in range(4, 8):
+        todo.append((do_em, (k,)))
+
+    def filler(n):
+        for _i in range(n):
+            if todo:
+                f, args = todo.pop(0)
+                f(*args)
+
+    wait("v", "act", max(a_tab, a_vr))
+    wait("v", "vec", v_off)
+    v_sc = 0
+    for t, s in enumerate(chain):
+        x = _pos(t)
+        win = T.tab[:, 0:C + CAP]
+        off = T.off4[:, 4 * s:4 * s + 3]
+        if t:
+            wait("v", "vec", v_sc)
+            v_pv = V(ve.tensor_copy(T.pv[:, x:x + CAP], win.indirect(off)))
+            filler(1 if t < 6 else 2)
+            wait("v", "vec", v_pv)
+        v_sc = V(ve.tensor_copy(win.indirect(off), T.vr[:, x:x + CAP]))
+        filler(2)
+    filler(len(todo))
+    wait("y", "vec", v_sc)
+    for k in range(8):
+        inc("dwrap", sy.dma_start(T.tw[16 * k:16 * k + 16, :], T.tab[16 * k:16 * k + 1, 0:C]), 16)
+
+    wait("v", "act", a_mk)
+    wait("v", "vec", v_pv)
+    v1 = V(ve.tensor_tensor_scan(T.sc1[:], T.pv[:], T.mk[:], 0.0, Op.add, Op.mult))
+    wait("v", "vec", v1)
+    v1 = V(ve.tensor_tensor_scan(T.sc2[:], T.seg[:], T.sc1[:], 0.0, Op.mult, Op.add))
+    wait("v", "vec", v1)
+    gw = T.sc2[:, 15:ALL:16]
+    V(ve.tensor_tensor(T.fs[:, 0:25], T.vw[:, 0:25], gw, Op.min))
+    v1 = V(ve.tensor_tensor(T.fs[:, 26:51], T.vw[:, 0:25], gw, Op.max))
+    wait("v", "vec", v1)
+    v1 = V(ve.tensor_scalar(T.fa[:], T.fs[:], KEY - 1, None, Op.bitwise_and))
+    wait("v", "vec", v1)
+    v_fsl = V(ve.tensor_scalar(T.fsl[:], T.fa[:], float(NEW), float(NEW), Op.max, Op.subtract))
+
+    wait("v", "dwc", cnt["dwc"])
+    v_ws = pickc(T.wselq, 0, ALL, T.wq, 0, C, T.wl, 0, 25)
+    wait("s", "dws", cnt["dws"])
+    wait("s", "vec", late["wl"])
+    a_ws = picks(T.wsels, 0, ALL, T.wqs, 0, C, T.wl, 0, 25)
+
+    def prod(ps, b, k, q, s, a, n, start, stop):
+        return te.matmul_mx(T[ps][:, 512 * b:512 * b + n], T.eq[:, 128 * k:128 * k + 128],
+                            T.es[:, 128 * k:128 * k + 128], T[q][:, a:a + n], T[s][:, a:a + n], start, stop)
+
+    parts = (("psa", 0, NA), ("psb", B0, NB))
+    wait("t", "vec", max(v_ws, v_ep))
+    wait("t", "act", a_ws)
+    for ps, a, n in parts:
+        for b in range(4):
+            prod(ps, b, b, "wselq", "wsels", a, n, True, False)
+
+    def arrived(stage):
+        return sum(len(_engines(s, _stages(s, pairs)[stage], T, topo)[me])
+                   for s in range(N) if s != me and me in _stages(s, pairs)[stage])
+
+    stops = []
+    for i, (ps, a, n) in enumerate(parts):
+        w1 = ZERO + (NA if i == 0 else ALL)
+        wait("v", "arrec" if i == 0 else "arrlc", arrived(i))
+        wait("s", "arres" if i == 0 else "arrls", arrived(i))
+        wait("v", "vec", max(v_fsl, v_own, v_zq))
+        wait("s", "vec", max(v_fsl, v_zq))
+        wait("s", "act", a_own)
+        o = a // 16
+        for q, s, o0, last in (("firq", "firs", o, False), ("secq", "secs", 26 + o, True)):
+            vp = pickc(T[q], a, a + n, T.landq, 0, w1, T.fsl, o0, o0 + n // 16)
+            ap = picks(T[s], a, a + n, T.lands, 0, w1, T.fsl, o0, o0 + n // 16)
+            wait("t", "vec", max(vp, late["em"]))
+            wait("t", "act", ap)
+            for b in range(4):
+                ins = prod(ps, b, 4 + b, q, s, a, n, False, last)
+                if last:
+                    stops.append(inc("ten", ins))
+        if i == 0:
+            wait("v", "dwrap", cnt["dwrap"])
+            v1 = V(ve.tensor_copy(T.ti[:], T.tw[:]))
+            wait("v", "vec", v1)
+            v1 = V(ve.tensor_scalar(T.tf[:], T.ti[:], KEY - 1, None, Op.bitwise_and))
+            wait("v", "vec", v1)
+            v_up = V(ve.tensor_scalar(T.upl[:], T.tf[:], float(NEW + ZERO - 16), float(NEW + ZERO - 16),
+                                      Op.max, Op.subtract))
+            v_fin = V(ve.tensor_copy(T.finl[:], T.tf[:]))
+            wait("s", "vec", v_pv)
+            a1 = A(sc.activation(T.hup[:, 16:16 + ALL], T.pv[:], Fn.Sign, bias=float(NONE - KEY // 8), scale=-1.0))
+            wait("s", "act", a1)
+            wait("s", "vec", v_up)
+            a_up = A(sc.activation(T.upr[:], T.hup[:].indirect(T.upl[:]), Fn.Identity, bias=1.5, scale=0.5))
+            wait("y", "act", a_up)
+            inc("dout", sy.dma_start(T.up[:], T.upr[0:1, :]), 16)
+
+    for i, (ps, a, n) in enumerate(parts):
+        vl = al = 0
+        for b in range(4):
+            out, src = T.h[:, 4 * a + b:4 * (a + n):4], T[ps][:, 512 * b:512 * b + n]
+            if b % 2 == 0:
+                wait("v", "ten", stops[4 * i + b])
+                vl = V(ve.tensor_copy(out, src))
+            else:
+                wait("s", "ten", stops[4 * i + b])
+                al = A(sc.activation(out, src, Fn.Copy))
+        wait("v", "vec", vl)
+        wait("v", "act", al)
+        x = NEW + ZERO + a
+        v_q = V(ve.quantize_mx(T.finq[:, x:x + n], T.fins[:, x:x + n], T.h[:, 4 * a:4 * (a + n)]))
+
+    wait("v", "vec", max(v_q, v_fin))
+    wait("v", "dfq", cnt["dfq"])
+    wait("s", "vec", max(v_q, v_fin))
+    wait("s", "dfs", cnt["dfs"])
+    W = NEW + ZERO + ALL
+    for j in range(4):
+        vp = pickc(T.outq, 256 * j, 256 * j + 256, T.finq, 0, W, T.finl, 16 * j, 16 * j + 16)
+        ap = picks(T.outs, 256 * j, 256 * j + 256, T.fins, 0, W, T.finl, 16 * j, 16 * j + 16)
+        wait("y", "vec", vp)
+        inc("dout", sy.dma_start(T.oc[:, 1024 * j:1024 * j + 1024], T.outq[:, 256 * j:256 * j + 256].bitcast(u8)), 16)
+    wait("s", "act", ap)
+    wait("y", "act", ap)
+    for k in range(4):
+        inc("dout", (sc if k < 2 else sy).dma_start(T.osc[4 * k:4 * k + 4, :], T.outs[32 * k:32 * k + 4, :]), 16)
+
+    wait("g", "sent", sent)
+    for name in ("vec", "act", "ten", "gpc", "dout"):
+        wait("g", name, cnt[name])

@@ -8,6 +8,7 @@ NEW = 1024
 ZERO = 128
 NA, NB, B0 = 240, 144, 256
 ALL = B0 + NB
+PARTS = (("psa", 0, NA, 0, 16, 32), ("psb", B0, ALL, 32, 42, 52))
 
 E4, U8, F32, I32, U16, BF = "float8_e4m3fn_x4", "uint8", "float32", "int32", "uint16", "bfloat16"
 
@@ -33,34 +34,26 @@ SCRATCH = {
     "tcw": _sb(24, I32), "ta": _sb(24, I32), "tb": _sb(24, I32), "tx": _sb(24, I32), "ty": _sb(24, I32),
     "tz": _sb(24, I32),
     "off4": _sb(32, U16), "wl": _sb(26, U16), "fsl": _sb(52, U16), "finl": _sb(64, U16), "upl": _sb(64, U16),
+    "upg": _sb(16, U16),
     "pidx": _sb(2, I32), "pa": _sb(2, I32), "pcol": _sb(4, F32),
     "m16": _sb(16, I32), "m16a": _sb(16, I32), "mk": _sb(ALL, F32), "seg": _sb(ALL, F32),
     "vb": _sb(26, F32), "vw": _sb(26, F32), "cb": _sb(24, F32), "cl": _sb(24, F32),
     "b48": _sb(48, F32), "vr": _sb(ALL, F32), "tab": _sb(C + CAP, F32), "pv": _sb(ALL, F32),
     "sc1": _sb(ALL, F32), "sc2": _sb(ALL, F32), "fs": _sb(52, I32), "fa": _sb(52, I32),
     "tw": _sb(64, F32), "ti": _sb(64, I32), "tf": _sb(64, I32),
-    "hup": _sb(16 + ALL, F32), "upr": _sb(C, F32),
+    "hup": _sb(16 + ALL, F32), "upr": _sb(256, F32),
     "psa": ("psum", [128, 2048], F32), "psb": ("psum", [128, 2048], F32),
 }
-SEMAPHORES = ["vec", "act", "ten", "gpc", "dsn", "dgr", "dtc", "dwc", "dws", "dfq", "dfs", "dwrap", "dout",
+SEMAPHORES = ["vec", "act", "ten", "gpc", "dsn", "dgr", "dtc", "dwc", "dws", "dfin", "dwrap", "dup", "dout",
               "arrec", "arres", "arrlc", "arrls", "sent", "issued"]
 
 
-def _pairs(T, topo):
-    out = []
-    for r in range(N):
-        if not any(r in p for p in out):
-            out.append([x for x in range(N)
-                        if x == r or topo.mates(topo.chip(T.cores[r]), topo.chip(T.cores[x]))])
-    return out
+def _stages(s):
+    return [(s + i) % N for i in range(1, 5)], [(s + i) % N for i in range(5, N)]
 
 
-def _stages(s, pairs):
-    u = [i for i, p in enumerate(pairs) if s in p][0]
-    n = len(pairs)
-    one = sorted(pairs[(u + 1) % n] + pairs[(u + 2) % n])
-    two = sorted(pairs[(u + 3) % n] + [x for x in pairs[u] if x != s])
-    return one, two
+def _chain(q):
+    return [(q - 4 + t) % N for t in range(N)]
 
 
 def _engines(s, stage, T, topo):
@@ -79,12 +72,6 @@ def _engines(s, stage, T, topo):
         out[q] = topo.engines(src, T.cores[q])[at:at + n]
         at += n
     return out
-
-
-def _chain(q, pairs):
-    early = [s for s in range(N) if s != q and q in _stages(s, pairs)[0]]
-    late = [s for s in range(N) if s != q and q in _stages(s, pairs)[1]]
-    return [q] + early + late
 
 
 def _pos(t):
@@ -128,29 +115,35 @@ def rank_program(g, core, T, topo):
             seen[(qn, name)] = val
             {"v": ve, "s": sc, "t": te, "y": sy, "g": g}[qn].wait_ge(sem[name], val)
 
-    pairs = _pairs(T, topo)
-    one, two = _stages(me, pairs)
-    chain = _chain(me, pairs)
+    def iota(out, pattern, base):
+        return G(g.iota(out, pattern, base, 0, allow_small_or_imprecise_dtypes=True))
+
+    one, two = _stages(me)
+    chain = _chain(me)
+    halves = ((0, chain[:5]), (16, chain[5:]))
     u8, u32 = dt.uint8, dt.uint32
 
+    for k in range(8):
+        inc("dsn", (sc if k < 4 else sy).dma_start(T.snw[16 * k:16 * k + 16, :], T.sn[:]), 16)
     inc("dgr", sy.dma_start(T.grt[:], T.gr[:]), 16)
     for k in range(8):
-        inc("dsn", (sc if k < 5 else sy).dma_start(T.snw[16 * k:16 * k + 16, :], T.sn[:]), 16)
-    for k in range(8):
-        inc("dtc", (sc if k < 3 else sy).dma_start(T.tcw[16 * k:16 * k + 16, :], T.tc[:]), 16)
+        inc("dtc", (sc if k < 4 else sy).dma_start(T.tcw[16 * k:16 * k + 16, :], T.tc[:]), 16)
     inc("dwc", sy.dma_start(T.wq[:].bitcast(u8), T.wc[:]), 16)
     inc("dws", sc.dma_start(T.wqs[:], T.ws[:]), 16)
 
     v_eo = V(ve.memset(T.eo[:], 1.0))
     v_zt = V(ve.memset(T.zt[:], 0.0))
-    p_tab = G(g.iota(T.tab[:, 0:64], [[16, 64]], NONE, 0, allow_small_or_imprecise_dtypes=True))
-    p_b48 = G(g.iota(T.b48[:], [[1, 48]], 0, 0, allow_small_or_imprecise_dtypes=True))
-    p_m16 = G(g.iota(T.m16[:], [[1, 16]], 128, -1))
-    p_idx = G(g.iota(T.pidx[:], [[0, 2]], 0, 1))
-    p_cb = G(g.iota(T.cb[:], [[0, 8], [16, 3]], C, 0, allow_small_or_imprecise_dtypes=True))
-    p_vb = G(g.iota(T.vb[:, 0:25], [[16, 25]], NEW + ZERO, 0, allow_small_or_imprecise_dtypes=True))
+    p_tab = iota(T.tab[:, 0:64], [[16, 64]], NONE)
     wait("g", "vec", v_eo)
     p_ef = G(g.affine_select(T.ef[:], T.eo[:], [[1, 516]], Op.is_equal, 0.0, -3, -4))
+    p_m16 = G(g.iota(T.m16[:], [[1, 16]], 128, -1))
+    p_idx = G(g.iota(T.pidx[:], [[0, 2]], 0, 1))
+    p_cb = iota(T.cb[:], [[0, 8], [16, 3]], C)
+    p_b48 = iota(T.b48[:], [[1, 48]], 0)
+    for base, ranks in halves:
+        for i, r, n in _runs(ranks):
+            c = base + 3 * i
+            p_vb = iota(T.vb[:, c:c + 3 * n], [[KEY + CAP, n], [16, 3]], KEY * r + NEW + ZERO + 16 * c)
 
     wait("s", "gpc", p_tab)
     a_tab = 0
@@ -158,6 +151,8 @@ def rank_program(g, core, T, topo):
         if a_tab:
             wait("s", "act", a_tab)
         a_tab = A(sc.activation(T.tab[:, 64 * r:128 * r], T.tab[:, 0:64 * r], Fn.Identity, bias=float(r)))
+    wait("s", "gpc", p_ef)
+    a_en = A(sc.activation(T.en[:], T.ef[:], Fn.Copy, scale=-0.125))
     wait("s", "gpc", p_b48)
     for t, s in enumerate(chain):
         x = _pos(t)
@@ -167,29 +162,13 @@ def rank_program(g, core, T, topo):
     V(ve.memset(T.pv[:, NA:B0], float(NONE)))
     V(ve.memset(T.tab[:, C:C + CAP], float(NONE)))
     V(ve.memset(T.fs[:], 0))
-    V(ve.memset(T.wl[:], 0))
+    v_vb = V(ve.memset(T.vb[:, 15:16], 0.0))
+    V(ve.memset(T.hup[:, 0:16], -3.0))
+    v_seg = V(ve.memset(T.seg[:], 1.0))
     wait("v", "vec", v_zt)
     v_zq = V(ve.quantize_mx(T.landq[:, 0:ZERO], T.lands[:, 0:ZERO], T.zt[:]))
-    wait("v", "gpc", p_m16)
-    v = V(ve.tensor_scalar(T.m16a[:], T.m16[:], 15, None, Op.bitwise_and))
-    wait("v", "gpc", p_idx)
-    v_pa = V(ve.tensor_scalar(T.pa[:], T.pidx[:], 15, None, Op.bitwise_and))
-    wait("v", "vec", v)
-    v_mk = V(ve.tensor_scalar(T.mk[:, 0:16], T.m16a[:], 0.0, None, Op.is_equal))
-    wait("v", "vec", v_pa)
-    v_pc = V(ve.tensor_copy(T.pcol[:, 0:1], T.pa[:, 0:1]))
-    wait("v", "gpc", p_cb)
-    wait("v", "vec", v_pc)
-    V(ve.tensor_scalar(T.cl[:], T.cb[:], T.pcol[:, 0:1], None, Op.add))
-
-    wait("s", "vec", v_mk)
-    a_mk, n = 0, 16
-    while n < ALL:
-        m = min(n, ALL - n)
-        if a_mk:
-            wait("s", "act", a_mk)
-        a_mk = A(sc.activation(T.mk[:, n:n + m], T.mk[:, 0:m], Fn.Copy))
-        n += m
+    wait("v", "vec", v_seg)
+    V(ve.memset(T.seg[:, 0:ALL:16], 0.0))
 
     def unit(k, src):
         b = k % 4
@@ -199,11 +178,22 @@ def rank_program(g, core, T, topo):
     wait("v", "gpc", p_ef)
     for k in range(4):
         v_ep = unit(k, T.ef)
+    wait("v", "gpc", p_m16)
+    v = V(ve.tensor_scalar(T.m16a[:], T.m16[:], 15, None, Op.bitwise_and))
+    wait("v", "gpc", p_idx)
+    v_pa = V(ve.tensor_scalar(T.pa[:], T.pidx[:], 15, None, Op.bitwise_and))
+    wait("v", "vec", v)
+    v_mk = V(ve.tensor_scalar(T.mk[:, 0:16], T.m16a[:], 0.0, None, Op.is_equal))
+    wait("v", "vec", v_pa)
+    v_pc = V(ve.tensor_copy(T.pcol[:, 0:1], T.pa[:, 0:1]))
 
     wait("v", "dsn", cnt["dsn"])
     for base, ranks in ((0, one), (12, two), (22, [me])):
         for i, r, n in _runs(ranks):
             V(ve.tensor_copy(T.soff[:, base + 3 * i:base + 3 * (i + n)], T.snw[:, 3 * r:3 * (r + n)]))
+    wait("v", "gpc", p_cb)
+    wait("v", "vec", v_pc)
+    v_cl = V(ve.tensor_scalar(T.cl[:], T.cb[:], T.pcol[:, 0:1], None, Op.add))
     wait("v", "dgr", cnt["dgr"])
     v_gq = V(ve.quantize_mx(T.gq[:], T.gs[:], T.grt[:]))
 
@@ -216,13 +206,23 @@ def rank_program(g, core, T, topo):
     wait("v", "vec", v_gq)
     wait("s", "vec", v_gq)
     n1, n2 = CAP * len(one), CAP * (len(one) + len(two))
-    sends = []
-    for stage, a, b, o0, o1, cs, ss in ((one, 0, n1, 0, 12, "arrec", "arres"), (two, n1, n2, 12, 21, "arrlc", "arrls")):
-        vp = pickc(T.slotq, a, b, T.gq, 0, S, T.soff, o0, o1)
-        ap = picks(T.slots, a, b, T.gs, 0, S, T.soff, o0, o1)
-        sends.append((stage, a, vp, ap, cs, ss))
+    own = ZERO + _pos(chain.index(me))
+    v_p1 = pickc(T.slotq, 0, n1, T.gq, 0, S, T.soff, 0, 12)
+    a_p1 = picks(T.slots, 0, n1, T.gs, 0, S, T.soff, 0, 12)
+    wait("v", "dtc", cnt["dtc"])
+    v_ta = V(ve.tensor_scalar(T.ta[:], T.tcw[:], 15, None, Op.bitwise_and))
+    v_p2 = pickc(T.slotq, n1, n2, T.gq, 0, S, T.soff, 12, 21)
+    a_p2 = picks(T.slots, n1, n2, T.gs, 0, S, T.soff, 12, 21)
+    V(ve.tensor_scalar(T.tb[:], T.tcw[:], 2047, 4, Op.bitwise_and, Op.logical_shift_right))
+    wait("v", "vec", v_ta)
+    v_tx = V(ve.tensor_scalar(T.tx[:], T.ta[:], 64.0, None, Op.mult))
+    v_own = pickc(T.landq, own, own + CAP, T.gq, 0, S, T.soff, 22, 25)
+    a_own = picks(T.lands, own, own + CAP, T.gs, 0, S, T.soff, 22, 25)
+    wait("v", "vec", v_tx)
+    v_ty = V(ve.tensor_tensor(T.ty[:], T.tx[:], T.tb[:], Op.add))
+
     sent = 0
-    for stage, a, vp, ap, cs, ss in sends:
+    for stage, a, vp, ap, cs, ss in ((one, 0, v_p1, a_p1, "arrec", "arres"), (two, n1, v_p2, a_p2, "arrlc", "arrls")):
         eng = _engines(me, stage, T, topo)
         for codes in (True, False):
             wait("g", "vec" if codes else "act", vp if codes else ap)
@@ -230,7 +230,7 @@ def rank_program(g, core, T, topo):
             for i, q in enumerate(stage):
                 rid, pid, _se = topo.addr(T.cores[q])
                 x = a + CAP * i
-                y = ZERO + _pos(_chain(q, pairs).index(me))
+                y = ZERO + _pos(_chain(q).index(me))
                 src, dst = ((T.slotq[:, x:x + CAP].bitcast(u8), T.landq[:, y:y + CAP].bitcast(u8)) if codes
                             else (T.slots[:, x:x + CAP], T.lands[:, y:y + CAP]))
                 tr.append(RemoteDMATransfer(dst_ids=[DstId(rid=rid, pnc=pid)],
@@ -241,67 +241,80 @@ def rank_program(g, core, T, topo):
     g.sem_inc(sem["issued"], 1)
 
     wait("y", "issued", 1)
-    inc("dfq", sy.dma_start(T.finq[:, 0:C].bitcast(u8), T.wc[:]), 16)
-    inc("dfs", sy.dma_start(T.fins[:, 0:C], T.ws[:]), 16)
+    inc("dfin", sy.dma_start(T.finq[:, 0:C // 2].bitcast(u8), T.wc[:, 0:2 * C]), 16)
 
-    v_own = pickc(T.landq, ZERO, ZERO + CAP, T.gq, 0, S, T.soff, 22, 25)
-    a_own = picks(T.lands, ZERO, ZERO + CAP, T.gs, 0, S, T.soff, 22, 25)
-
-    wait("v", "dtc", cnt["dtc"])
-    v1 = V(ve.tensor_scalar(T.ta[:], T.tcw[:], 15, None, Op.bitwise_and))
-    V(ve.tensor_scalar(T.tb[:], T.tcw[:], 2047, 4, Op.bitwise_and, Op.logical_shift_right))
-    wait("v", "vec", v1)
-    v1 = V(ve.tensor_scalar(T.tx[:], T.ta[:], 64.0, None, Op.mult))
-    wait("v", "vec", v1)
-    v1 = V(ve.tensor_tensor(T.ty[:], T.tx[:], T.tb[:], Op.add))
-    wait("v", "vec", v1)
-    v1 = V(ve.tensor_tensor(T.tz[:], T.ty[:], T.cl[:], Op.min))
-    wait("v", "vec", v1)
-    for i in range(3):
-        v_off = V(ve.tensor_copy(T.off4[:, i:32:4], T.tz[:, i:24:3]))
+    wait("s", "vec", v_mk)
+    a_mk, n = 0, 16
+    while n < ALL:
+        m = min(n, ALL - n)
+        if a_mk:
+            wait("s", "act", a_mk)
+        a_mk = A(sc.activation(T.mk[:, n:n + m], T.mk[:, 0:m], Fn.Copy))
+        n += m
+    wait("s", "gpc", p_vb)
+    wait("s", "vec", max(v_pc, v_vb))
+    a_vw = A(sc.activation(T.vw[:, 0:25], T.vb[:, 0:25], Fn.Identity, bias=T.pcol[:, 0:1]))
 
     late, todo = {}, []
 
     def do_wl(a, b, x, y):
         late["wl"] = V(ve.tensor_copy(T.wl[:, a:b], T.tcw[:, x:y]))
 
-    def do_vw(c, n, key):
-        wait("v", "gpc", p_vb)
-        late["vw"] = V(ve.tensor_scalar(T.vw[:, c:c + n], T.vb[:, c:c + n], T.pcol[:, 0:1], float(key), Op.add, Op.add))
-
-    def do_seg(start):
-        if start:
-            late["seg"] = V(ve.memset(T.seg[:], 1.0))
-        else:
-            wait("v", "vec", late["seg"])
-            V(ve.memset(T.seg[:, 0:ALL:16], 0.0))
-
-    def do_en():
-        late["en"] = V(ve.tensor_scalar(T.en[:], T.ef[:], -0.125, None, Op.mult))
-
     def do_em(k):
-        wait("v", "vec", late["en"])
+        wait("v", "act", a_en)
         late["em"] = unit(k, T.en)
 
-    for base, ranks in ((0, chain[:5]), (16, chain[5:])):
+    def do_w(a, b):
+        wait("v", "dwc", cnt["dwc"])
+        wait("v", "vec", late["wl"])
+        wait("s", "dws", cnt["dws"])
+        wait("s", "vec", late["wl"])
+        late["w"] = pickc(T.wselq, a, b, T.wq, 0, C, T.wl, a // 16, b // 16)
+        late["ws"] = picks(T.wsels, a, b, T.wqs, 0, C, T.wl, a // 16, b // 16)
+
+    def do_list(part, step):
+        _ps, a, z, x, y, e = part
+        key, n = ("list", a), (z - a) // 16
+        if step == 0:
+            wait("v", "act", a_mk)
+            wait("v", "vec", late["pv"])
+            late[key] = V(ve.tensor_tensor_scan(T.sc1[:, a:z], T.pv[:, a:z], T.mk[:, a:z], 0.0, Op.add, Op.mult))
+            return
+        wait("v", "vec", late[key])
+        if step == 1:
+            late[key] = V(ve.tensor_tensor_scan(T.sc2[:, a:z], T.seg[:, a:z], T.sc1[:, a:z], 0.0, Op.mult, Op.add))
+        elif step == 2:
+            wait("v", "act", a_vw)
+            gw, mine = T.sc2[:, a + 15:z:16], T.vw[:, a // 16:z // 16]
+            V(ve.tensor_tensor(T.fs[:, x:x + n], mine, gw, Op.min))
+            late[key] = V(ve.tensor_tensor(T.fs[:, y:y + n], mine, gw, Op.max))
+        elif step == 3:
+            late[key] = V(ve.tensor_scalar(T.fa[:, x:e], T.fs[:, x:e], KEY - 1, None, Op.bitwise_and))
+        else:
+            late[key] = V(ve.tensor_scalar(T.fsl[:, x:e], T.fa[:, x:e], float(NEW), float(NEW), Op.max, Op.subtract))
+
+    for base, ranks in halves:
         for i, r, n in _runs(ranks):
             todo.append((do_wl, (base + 3 * i, base + 3 * (i + n), 3 * r, 3 * (r + n))))
-    todo.append((do_seg, (True,)))
-    for k, s in enumerate(chain):
-        todo.append((do_vw, (_pos(k) // 16, 3, KEY * s)))
-    todo.append((do_vw, (15, 1, 0)))
-    todo.append((do_seg, (False,)))
-    todo.append((do_en, ()))
-    todo.append((lambda: V(ve.memset(T.hup[:, 0:16], -3.0)), ()))
     for k in range(4, 8):
         todo.append((do_em, (k,)))
+    todo.append((do_w, (0, NA)))
+    todo.append((do_w, (B0, ALL)))
 
-    def filler(n):
+    def filler(n=1):
         for _i in range(n):
             if todo:
                 f, args = todo.pop(0)
                 f(*args)
 
+    filler()
+    wait("v", "vec", max(v_ty, v_cl))
+    v_tz = V(ve.tensor_tensor(T.tz[:], T.ty[:], T.cl[:], Op.min))
+    filler()
+    wait("v", "vec", v_tz)
+    for i in range(3):
+        v_off = V(ve.tensor_copy(T.off4[:, i:32:4], T.tz[:, i:24:3]))
+    filler()
     wait("v", "act", max(a_tab, a_vr))
     wait("v", "vec", v_off)
     v_sc = 0
@@ -311,115 +324,109 @@ def rank_program(g, core, T, topo):
         off = T.off4[:, 4 * s:4 * s + 3]
         if t:
             wait("v", "vec", v_sc)
-            v_pv = V(ve.tensor_copy(T.pv[:, x:x + CAP], win.indirect(off)))
-            filler(1 if t < 6 else 2)
-            wait("v", "vec", v_pv)
+            late["pv"] = V(ve.tensor_copy(T.pv[:, x:x + CAP], win.indirect(off)))
+            if t == 4:
+                filler(len(todo))
+                todo.extend((do_list, (PARTS[0], k)) for k in range(5))
+            else:
+                filler()
+            wait("v", "vec", late["pv"])
         v_sc = V(ve.tensor_copy(win.indirect(off), T.vr[:, x:x + CAP]))
-        filler(2)
+        if t:
+            filler()
     filler(len(todo))
     wait("y", "vec", v_sc)
     for k in range(8):
         inc("dwrap", sy.dma_start(T.tw[16 * k:16 * k + 16, :], T.tab[16 * k:16 * k + 1, 0:C]), 16)
+    inc("dfin", sy.dma_start(T.finq[:, C // 2:C].bitcast(u8), T.wc[:, 2 * C:4 * C]), 16)
+    inc("dfin", sy.dma_start(T.fins[:, 0:C], T.ws[:]), 16)
+    for k in range(5):
+        do_list(PARTS[1], k)
+    wait("s", "vec", late["pv"])
+    a_h = A(sc.activation(T.hup[:, 16:16 + ALL], T.pv[:], Fn.Sign, bias=float(NONE - KEY // 8), scale=-1.0))
 
-    wait("v", "act", a_mk)
-    wait("v", "vec", v_pv)
-    v1 = V(ve.tensor_tensor_scan(T.sc1[:], T.pv[:], T.mk[:], 0.0, Op.add, Op.mult))
-    wait("v", "vec", v1)
-    v1 = V(ve.tensor_tensor_scan(T.sc2[:], T.seg[:], T.sc1[:], 0.0, Op.mult, Op.add))
-    wait("v", "vec", v1)
-    gw = T.sc2[:, 15:ALL:16]
-    V(ve.tensor_tensor(T.fs[:, 0:25], T.vw[:, 0:25], gw, Op.min))
-    v1 = V(ve.tensor_tensor(T.fs[:, 26:51], T.vw[:, 0:25], gw, Op.max))
-    wait("v", "vec", v1)
-    v1 = V(ve.tensor_scalar(T.fa[:], T.fs[:], KEY - 1, None, Op.bitwise_and))
-    wait("v", "vec", v1)
-    v_fsl = V(ve.tensor_scalar(T.fsl[:], T.fa[:], float(NEW), float(NEW), Op.max, Op.subtract))
+    def prod(ps, b, k, q, s, a, z, start, stop):
+        return te.matmul_mx(T[ps][:, 512 * b:512 * b + z - a], T.eq[:, 128 * k:128 * k + 128],
+                            T.es[:, 128 * k:128 * k + 128], T[q][:, a:z], T[s][:, a:z], start, stop)
 
-    wait("v", "dwc", cnt["dwc"])
-    v_ws = pickc(T.wselq, 0, ALL, T.wq, 0, C, T.wl, 0, 25)
-    wait("s", "dws", cnt["dws"])
-    wait("s", "vec", late["wl"])
-    a_ws = picks(T.wsels, 0, ALL, T.wqs, 0, C, T.wl, 0, 25)
-
-    def prod(ps, b, k, q, s, a, n, start, stop):
-        return te.matmul_mx(T[ps][:, 512 * b:512 * b + n], T.eq[:, 128 * k:128 * k + 128],
-                            T.es[:, 128 * k:128 * k + 128], T[q][:, a:a + n], T[s][:, a:a + n], start, stop)
-
-    parts = (("psa", 0, NA), ("psb", B0, NB))
-    wait("t", "vec", max(v_ws, v_ep))
-    wait("t", "act", a_ws)
-    for ps, a, n in parts:
+    wait("t", "vec", max(late["w"], v_ep))
+    wait("t", "act", late["ws"])
+    for ps, a, z, _x, _y, _e in PARTS:
         for b in range(4):
-            prod(ps, b, b, "wselq", "wsels", a, n, True, False)
+            prod(ps, b, b, "wselq", "wsels", a, z, True, False)
 
     def arrived(stage):
-        return sum(len(_engines(s, _stages(s, pairs)[stage], T, topo)[me])
-                   for s in range(N) if s != me and me in _stages(s, pairs)[stage])
+        return sum(len(_engines(s, _stages(s)[stage], T, topo)[me])
+                   for s in range(N) if s != me and me in _stages(s)[stage])
 
     stops = []
-    for i, (ps, a, n) in enumerate(parts):
-        w1 = ZERO + (NA if i == 0 else ALL)
+    for i, (ps, a, z, x, y, e) in enumerate(PARTS):
+        w1, n = ZERO + z, (z - a) // 16
         wait("v", "arrec" if i == 0 else "arrlc", arrived(i))
         wait("s", "arres" if i == 0 else "arrls", arrived(i))
-        wait("v", "vec", max(v_fsl, v_own, v_zq))
-        wait("s", "vec", max(v_fsl, v_zq))
+        wait("v", "vec", max(late["list", a], v_own, v_zq))
+        wait("s", "vec", max(late["list", a], v_zq))
         wait("s", "act", a_own)
-        o = a // 16
-        for q, s, o0, last in (("firq", "firs", o, False), ("secq", "secs", 26 + o, True)):
-            vp = pickc(T[q], a, a + n, T.landq, 0, w1, T.fsl, o0, o0 + n // 16)
-            ap = picks(T[s], a, a + n, T.lands, 0, w1, T.fsl, o0, o0 + n // 16)
+        for q, s, o, last in (("firq", "firs", x, False), ("secq", "secs", y, True)):
+            vp = pickc(T[q], a, z, T.landq, 0, w1, T.fsl, o, o + n)
+            ap = picks(T[s], a, z, T.lands, 0, w1, T.fsl, o, o + n)
             wait("t", "vec", max(vp, late["em"]))
             wait("t", "act", ap)
             for b in range(4):
-                ins = prod(ps, b, 4 + b, q, s, a, n, False, last)
+                ins = prod(ps, b, 4 + b, q, s, a, z, False, last)
                 if last:
                     stops.append(inc("ten", ins))
-        if i == 0:
-            wait("v", "dwrap", cnt["dwrap"])
-            v1 = V(ve.tensor_copy(T.ti[:], T.tw[:]))
-            wait("v", "vec", v1)
-            v1 = V(ve.tensor_scalar(T.tf[:], T.ti[:], KEY - 1, None, Op.bitwise_and))
-            wait("v", "vec", v1)
-            v_up = V(ve.tensor_scalar(T.upl[:], T.tf[:], float(NEW + ZERO - 16), float(NEW + ZERO - 16),
-                                      Op.max, Op.subtract))
-            v_fin = V(ve.tensor_copy(T.finl[:], T.tf[:]))
-            wait("s", "vec", v_pv)
-            a1 = A(sc.activation(T.hup[:, 16:16 + ALL], T.pv[:], Fn.Sign, bias=float(NONE - KEY // 8), scale=-1.0))
-            wait("s", "act", a1)
-            wait("s", "vec", v_up)
-            a_up = A(sc.activation(T.upr[:], T.hup[:].indirect(T.upl[:]), Fn.Identity, bias=1.5, scale=0.5))
-            wait("y", "act", a_up)
-            inc("dout", sy.dma_start(T.up[:], T.upr[0:1, :]), 16)
 
-    for i, (ps, a, n) in enumerate(parts):
+    wait("v", "dwrap", cnt["dwrap"])
+    v_ti = V(ve.tensor_copy(T.ti[:], T.tw[:]))
+
+    for i, (ps, a, z, _x, _y, _e) in enumerate(PARTS):
         vl = al = 0
         for b in range(4):
-            out, src = T.h[:, 4 * a + b:4 * (a + n):4], T[ps][:, 512 * b:512 * b + n]
+            out, src = T.h[:, 4 * a + b:4 * z:4], T[ps][:, 512 * b:512 * b + z - a]
             if b % 2 == 0:
                 wait("v", "ten", stops[4 * i + b])
                 vl = V(ve.tensor_copy(out, src))
+                if i == 0 and b == 0:
+                    wait("v", "vec", v_ti)
+                    v_tf = V(ve.tensor_scalar(T.tf[:], T.ti[:], KEY - 1, None, Op.bitwise_and))
             else:
                 wait("s", "ten", stops[4 * i + b])
                 al = A(sc.activation(out, src, Fn.Copy))
+        if i == 0:
+            wait("v", "vec", v_tf)
+            v_up = V(ve.tensor_scalar(T.upl[:], T.tf[:], float(NEW + ZERO - 16), float(NEW + ZERO - 16),
+                                      Op.max, Op.subtract))
+            v_fin = V(ve.tensor_copy(T.finl[:], T.tf[:]))
         wait("v", "vec", vl)
         wait("v", "act", al)
-        x = NEW + ZERO + a
-        v_q = V(ve.quantize_mx(T.finq[:, x:x + n], T.fins[:, x:x + n], T.h[:, 4 * a:4 * (a + n)]))
+        x = NEW + ZERO
+        v_q = V(ve.quantize_mx(T.finq[:, x + a:x + z], T.fins[:, x + a:x + z], T.h[:, 4 * a:4 * z]))
+
+    wait("y", "vec", v_up)
+    for k in range(8):
+        c = 16 * (k // 2)
+        inc("dup", sy.dma_start(T.upg[16 * k:16 * k + 16, :], T.upl[16 * k:16 * k + 16, c:c + 16]), 16)
 
     wait("v", "vec", max(v_q, v_fin))
-    wait("v", "dfq", cnt["dfq"])
+    wait("v", "dfin", cnt["dfin"])
     wait("s", "vec", max(v_q, v_fin))
-    wait("s", "dfs", cnt["dfs"])
+    wait("s", "dfin", cnt["dfin"])
     W = NEW + ZERO + ALL
     for j in range(4):
         vp = pickc(T.outq, 256 * j, 256 * j + 256, T.finq, 0, W, T.finl, 16 * j, 16 * j + 16)
         ap = picks(T.outs, 256 * j, 256 * j + 256, T.fins, 0, W, T.finl, 16 * j, 16 * j + 16)
         wait("y", "vec", vp)
         inc("dout", sy.dma_start(T.oc[:, 1024 * j:1024 * j + 1024], T.outq[:, 256 * j:256 * j + 256].bitcast(u8)), 16)
-    wait("s", "act", ap)
     wait("y", "act", ap)
     for k in range(4):
-        inc("dout", (sc if k < 2 else sy).dma_start(T.osc[4 * k:4 * k + 4, :], T.outs[32 * k:32 * k + 4, :]), 16)
+        inc("dout", sy.dma_start(T.osc[4 * k:4 * k + 4, :], T.outs[32 * k:32 * k + 4, :]), 16)
+    wait("s", "dup", cnt["dup"])
+    wait("s", "act", a_h)
+    a_up = A(sc.activation(T.upr[:], T.hup[:].indirect(T.upg[:]), Fn.Identity, bias=1.5, scale=0.5))
+    wait("s", "act", a_up)
+    for k in range(4):
+        inc("dout", sc.dma_start(T.up[:, 256 * k:256 * k + 256], T.upr[32 * k:32 * k + 1, :]), 16)
 
     wait("g", "sent", sent)
     for name in ("vec", "act", "ten", "gpc", "dout"):

from concourse.bass import DstId, RemoteDMATransfer
from concourse.mybir import dt, AluOpType as Op, ActivationFunctionType as Fn

C, S, CAP, N = 1024, 256, 48, 8
KEY = 2048
NONE = N * KEY
NEW = 1024
ZERO = 128
NA, NB, B0 = 240, 144, 256
ALL = B0 + NB
PARTS = (("psa", 0, NA, 0, 16, 32), ("psb", B0, ALL, 32, 42, 52))

E4, U8, F32, I32, U16, BF = "float8_e4m3fn_x4", "uint8", "float32", "int32", "uint16", "bfloat16"


def _sb(n, d):
    return ("sbuf", [128, n], d)


SCRATCH = {
    "grt": _sb(4 * S, BF), "gq": _sb(S, E4), "gs": _sb(S, U8),
    "snw": _sb(24, I32), "soff": _sb(26, U16),
    "slotq": _sb(336, E4), "slots": _sb(336, U8),
    "landq": _sb(ZERO + ALL, E4), "lands": _sb(ZERO + ALL, U8),
    "zt": _sb(512, BF), "eo": _sb(516, BF), "ef": _sb(516, BF), "en": _sb(516, BF),
    "eq": _sb(1024, E4), "es": _sb(1024, U8),
    "wq": _sb(C, E4), "wqs": _sb(C, U8),
    "finq": _sb(NEW + ZERO + ALL, E4), "fins": _sb(NEW + ZERO + ALL, U8),
    "wselq": _sb(ALL, E4), "wsels": _sb(ALL, U8),
    "firq": _sb(ALL, E4), "firs": _sb(ALL, U8),
    "secq": _sb(ALL, E4), "secs": _sb(ALL, U8),
    "h": _sb(4 * ALL, BF),
    "outq": _sb(C, E4), "outs": _sb(C, U8),
    "tcw": _sb(24, I32), "ta": _sb(24, I32), "tb": _sb(24, I32), "tx": _sb(24, I32), "ty": _sb(24, I32),
    "tz": _sb(24, I32),
    "off4": _sb(32, U16), "wl": _sb(26, U16), "fsl": _sb(52, U16), "finl": _sb(64, U16), "upl": _sb(64, U16),
    "upg": _sb(16, U16),
    "pidx": _sb(2, I32), "pa": _sb(2, I32), "pcol": _sb(4, F32),
    "m16": _sb(16, I32), "m16a": _sb(16, I32), "mk": _sb(ALL, F32), "seg": _sb(ALL, F32),
    "vb": _sb(26, F32), "vw": _sb(26, F32), "cb": _sb(24, F32), "cl": _sb(24, F32),
    "b48": _sb(48, F32), "vr": _sb(ALL, F32), "tab": _sb(C + CAP, F32), "pv": _sb(ALL, F32),
    "sc1": _sb(ALL, F32), "sc2": _sb(ALL, F32), "fs": _sb(52, I32), "fa": _sb(52, I32),
    "tw": _sb(64, F32), "ti": _sb(64, I32), "tf": _sb(64, I32),
    "hup": _sb(16 + ALL, F32), "upr": _sb(256, F32),
    "psa": ("psum", [128, 2048], F32), "psb": ("psum", [128, 2048], F32),
}
SEMAPHORES = ["vec", "act", "ten", "gpc", "dsn", "dgr", "dtc", "dwc", "dws", "dfin", "dwrap", "dup", "dout",
              "arrec", "arres", "arrlc", "arrls", "sent", "issued"]


def _stages(s):
    return [(s + i) % N for i in range(1, 5)], [(s + i) % N for i in range(5, N)]


def _chain(q):
    return [(q - 4 + t) % N for t in range(N)]


def _engines(s, stage, T, topo):
    src = T.cores[s]
    have = len(topo.engines(src, T.cores[stage[0]]))
    size = 1
    while 2 * size * len(stage) <= have:
        size *= 2
    spare = have - size * len(stage)
    out, at = {}, 0
    for q in stage:
        a, b = topo.chip(src), topo.chip(T.cores[q])
        n = size
        if spare >= size and not topo.mates(a, b) and not topo.same_plane(a, b):
            n, spare = 2 * size, spare - size
        out[q] = topo.engines(src, T.cores[q])[at:at + n]
        at += n
    return out


def _pos(t):
    return CAP * t if t < NA // CAP else CAP * t + B0 - NA


def _runs(ranks):
    out = []
    for i, r in enumerate(ranks):
        if out and out[-1][1] + out[-1][2] == r:
            out[-1][2] += 1
        else:
            out.append([i, r, 1])
    return out


def rank_program(g, core, T, topo):
    me = T.rank_of(core)
    if me is None:
        return
    sem = T.sem
    ve, sc, te, sy = g.vector, g.scalar, g.tensor, g.sync
    cnt, seen = {}, {}

    def inc(name, ins, by=1):
        ins.then_inc(sem[name], by)
        cnt[name] = cnt.get(name, 0) + by
        return cnt[name]

    def V(ins):
        return inc("vec", ins)

    def A(ins):
        return inc("act", ins)

    def G(ins):
        return inc("gpc", ins)

    def wait(qn, name, val):
        if seen.get((qn, name), 0) < val:
            seen[(qn, name)] = val
            {"v": ve, "s": sc, "t": te, "y": sy, "g": g}[qn].wait_ge(sem[name], val)

    def iota(out, pattern, base):
        return G(g.iota(out, pattern, base, 0, allow_small_or_imprecise_dtypes=True))

    one, two = _stages(me)
    chain = _chain(me)
    halves = ((0, chain[:5]), (16, chain[5:]))
    u8, u32 = dt.uint8, dt.uint32

    for k in range(8):
        inc("dsn", (sc if k < 4 else sy).dma_start(T.snw[16 * k:16 * k + 16, :], T.sn[:]), 16)
    inc("dgr", sy.dma_start(T.grt[:], T.gr[:]), 16)
    for k in range(8):
        inc("dtc", (sc if k < 4 else sy).dma_start(T.tcw[16 * k:16 * k + 16, :], T.tc[:]), 16)
    inc("dwc", sy.dma_start(T.wq[:].bitcast(u8), T.wc[:]), 16)
    inc("dws", sc.dma_start(T.wqs[:], T.ws[:]), 16)

    v_eo = V(ve.memset(T.eo[:], 1.0))
    v_zt = V(ve.memset(T.zt[:], 0.0))
    p_tab = iota(T.tab[:, 0:64], [[16, 64]], NONE)
    wait("g", "vec", v_eo)
    p_ef = G(g.affine_select(T.ef[:], T.eo[:], [[1, 516]], Op.is_equal, 0.0, -3, -4))
    p_m16 = G(g.iota(T.m16[:], [[1, 16]], 128, -1))
    p_idx = G(g.iota(T.pidx[:], [[0, 2]], 0, 1))
    p_cb = iota(T.cb[:], [[0, 8], [16, 3]], C)
    p_b48 = iota(T.b48[:], [[1, 48]], 0)
    for base, ranks in halves:
        for i, r, n in _runs(ranks):
            c = base + 3 * i
            p_vb = iota(T.vb[:, c:c + 3 * n], [[KEY + CAP, n], [16, 3]], KEY * r + NEW + ZERO + 16 * c)

    wait("s", "gpc", p_tab)
    a_tab = 0
    for r in (1, 2, 4, 8):
        if a_tab:
            wait("s", "act", a_tab)
        a_tab = A(sc.activation(T.tab[:, 64 * r:128 * r], T.tab[:, 0:64 * r], Fn.Identity, bias=float(r)))
    wait("s", "gpc", p_ef)
    a_en = A(sc.activation(T.en[:], T.ef[:], Fn.Copy, scale=-0.125))
    wait("s", "gpc", p_b48)
    for t, s in enumerate(chain):
        x = _pos(t)
        a_vr = A(sc.activation(T.vr[:, x:x + CAP], T.b48[:], Fn.Identity, bias=float(KEY * s + NEW + ZERO + x)))

    V(ve.memset(T.pv[:, 0:CAP], float(NONE)))
    V(ve.memset(T.pv[:, NA:B0], float(NONE)))
    V(ve.memset(T.tab[:, C:C + CAP], float(NONE)))
    V(ve.memset(T.fs[:], 0))
    v_vb = V(ve.memset(T.vb[:, 15:16], 0.0))
    V(ve.memset(T.hup[:, 0:16], -3.0))
    v_seg = V(ve.memset(T.seg[:], 1.0))
    wait("v", "vec", v_zt)
    v_zq = V(ve.quantize_mx(T.landq[:, 0:ZERO], T.lands[:, 0:ZERO], T.zt[:]))
    wait("v", "vec", v_seg)
    V(ve.memset(T.seg[:, 0:ALL:16], 0.0))

    def unit(k, src):
        b = k % 4
        return V(ve.quantize_mx(T.eq[:, 128 * k:128 * k + 128], T.es[:, 128 * k:128 * k + 128],
                                src[:, 3 - b:3 - b + 512]))

    wait("v", "gpc", p_ef)
    for k in range(4):
        v_ep = unit(k, T.ef)
    wait("v", "gpc", p_m16)
    v = V(ve.tensor_scalar(T.m16a[:], T.m16[:], 15, None, Op.bitwise_and))
    wait("v", "gpc", p_idx)
    v_pa = V(ve.tensor_scalar(T.pa[:], T.pidx[:], 15, None, Op.bitwise_and))
    wait("v", "vec", v)
    v_mk = V(ve.tensor_scalar(T.mk[:, 0:16], T.m16a[:], 0.0, None, Op.is_equal))
    wait("v", "vec", v_pa)
    v_pc = V(ve.tensor_copy(T.pcol[:, 0:1], T.pa[:, 0:1]))

    wait("v", "dsn", cnt["dsn"])
    for base, ranks in ((0, one), (12, two), (22, [me])):
        for i, r, n in _runs(ranks):
            V(ve.tensor_copy(T.soff[:, base + 3 * i:base + 3 * (i + n)], T.snw[:, 3 * r:3 * (r + n)]))
    wait("v", "gpc", p_cb)
    wait("v", "vec", v_pc)
    v_cl = V(ve.tensor_scalar(T.cl[:], T.cb[:], T.pcol[:, 0:1], None, Op.add))
    wait("v", "dgr", cnt["dgr"])
    v_gq = V(ve.quantize_mx(T.gq[:], T.gs[:], T.grt[:]))

    def pickc(out, a, b, win, w0, w1, off, o0, o1):
        return V(ve.tensor_copy(out[:, a:b].bitcast(u32), win[:, w0:w1].bitcast(u32).indirect(off[:, o0:o1])))

    def picks(out, a, b, win, w0, w1, off, o0, o1):
        return A(sc.activation(out[:, a:b], win[:, w0:w1].indirect(off[:, o0:o1]), Fn.Copy))

    wait("v", "vec", v_gq)
    wait("s", "vec", v_gq)
    n1, n2 = CAP * len(one), CAP * (len(one) + len(two))
    own = ZERO + _pos(chain.index(me))
    v_p1 = pickc(T.slotq, 0, n1, T.gq, 0, S, T.soff, 0, 12)
    a_p1 = picks(T.slots, 0, n1, T.gs, 0, S, T.soff, 0, 12)
    wait("v", "dtc", cnt["dtc"])
    v_ta = V(ve.tensor_scalar(T.ta[:], T.tcw[:], 15, None, Op.bitwise_and))
    v_p2 = pickc(T.slotq, n1, n2, T.gq, 0, S, T.soff, 12, 21)
    a_p2 = picks(T.slots, n1, n2, T.gs, 0, S, T.soff, 12, 21)
    V(ve.tensor_scalar(T.tb[:], T.tcw[:], 2047, 4, Op.bitwise_and, Op.logical_shift_right))
    wait("v", "vec", v_ta)
    v_tx = V(ve.tensor_scalar(T.tx[:], T.ta[:], 64.0, None, Op.mult))
    v_own = pickc(T.landq, own, own + CAP, T.gq, 0, S, T.soff, 22, 25)
    a_own = picks(T.lands, own, own + CAP, T.gs, 0, S, T.soff, 22, 25)
    wait("v", "vec", v_tx)
    v_ty = V(ve.tensor_tensor(T.ty[:], T.tx[:], T.tb[:], Op.add))

    sent = 0
    for stage, a, vp, ap, cs, ss in ((one, 0, v_p1, a_p1, "arrec", "arres"), (two, n1, v_p2, a_p2, "arrlc", "arrls")):
        eng = _engines(me, stage, T, topo)
        for codes in (True, False):
            wait("g", "vec" if codes else "act", vp if codes else ap)
            tr = []
            for i, q in enumerate(stage):
                rid, pid, _se = topo.addr(T.cores[q])
                x = a + CAP * i
                y = ZERO + _pos(_chain(q).index(me))
                src, dst = ((T.slotq[:, x:x + CAP].bitcast(u8), T.landq[:, y:y + CAP].bitcast(u8)) if codes
                            else (T.slots[:, x:x + CAP], T.lands[:, y:y + CAP]))
                tr.append(RemoteDMATransfer(dst_ids=[DstId(rid=rid, pnc=pid)],
                                            dma_engine_mask=sum(1 << e for e in eng[q]),
                                            remote_sem=sem[cs if codes else ss], src=src, dst=dst))
                sent += len(eng[q])
            g.remote_dma_fused(tr, local_sem=sem["sent"])
    g.sem_inc(sem["issued"], 1)

    wait("y", "issued", 1)
    inc("dfin", sy.dma_start(T.finq[:, 0:C // 2].bitcast(u8), T.wc[:, 0:2 * C]), 16)

    wait("s", "vec", v_mk)
    a_mk, n = 0, 16
    while n < ALL:
        m = min(n, ALL - n)
        if a_mk:
            wait("s", "act", a_mk)
        a_mk = A(sc.activation(T.mk[:, n:n + m], T.mk[:, 0:m], Fn.Copy))
        n += m
    wait("s", "gpc", p_vb)
    wait("s", "vec", max(v_pc, v_vb))
    a_vw = A(sc.activation(T.vw[:, 0:25], T.vb[:, 0:25], Fn.Identity, bias=T.pcol[:, 0:1]))

    late, todo = {}, []

    def do_wl(a, b, x, y):
        late["wl"] = V(ve.tensor_copy(T.wl[:, a:b], T.tcw[:, x:y]))

    def do_em(k):
        wait("v", "act", a_en)
        late["em"] = unit(k, T.en)

    def do_w(a, b):
        wait("v", "dwc", cnt["dwc"])
        wait("v", "vec", late["wl"])
        wait("s", "dws", cnt["dws"])
        wait("s", "vec", late["wl"])
        late["w"] = pickc(T.wselq, a, b, T.wq, 0, C, T.wl, a // 16, b // 16)
        late["ws"] = picks(T.wsels, a, b, T.wqs, 0, C, T.wl, a // 16, b // 16)

    def do_list(part, step):
        _ps, a, z, x, y, e = part
        key, n = ("list", a), (z - a) // 16
        if step == 0:
            wait("v", "act", a_mk)
            wait("v", "vec", late["pv"])
            late[key] = V(ve.tensor_tensor_scan(T.sc1[:, a:z], T.pv[:, a:z], T.mk[:, a:z], 0.0, Op.add, Op.mult))
            return
        wait("v", "vec", late[key])
        if step == 1:
            late[key] = V(ve.tensor_tensor_scan(T.sc2[:, a:z], T.seg[:, a:z], T.sc1[:, a:z], 0.0, Op.mult, Op.add))
        elif step == 2:
            wait("v", "act", a_vw)
            gw, mine = T.sc2[:, a + 15:z:16], T.vw[:, a // 16:z // 16]
            V(ve.tensor_tensor(T.fs[:, x:x + n], mine, gw, Op.min))
            late[key] = V(ve.tensor_tensor(T.fs[:, y:y + n], mine, gw, Op.max))
        elif step == 3:
            late[key] = V(ve.tensor_scalar(T.fa[:, x:e], T.fs[:, x:e], KEY - 1, None, Op.bitwise_and))
        else:
            late[key] = V(ve.tensor_scalar(T.fsl[:, x:e], T.fa[:, x:e], float(NEW), float(NEW), Op.max, Op.subtract))

    for base, ranks in halves:
        for i, r, n in _runs(ranks):
            todo.append((do_wl, (base + 3 * i, base + 3 * (i + n), 3 * r, 3 * (r + n))))
    for k in range(4, 8):
        todo.append((do_em, (k,)))
    todo.append((do_w, (0, NA)))
    todo.append((do_w, (B0, ALL)))

    def filler(n=1):
        for _i in range(n):
            if todo:
                f, args = todo.pop(0)
                f(*args)

    filler()
    wait("v", "vec", max(v_ty, v_cl))
    v_tz = V(ve.tensor_tensor(T.tz[:], T.ty[:], T.cl[:], Op.min))
    filler()
    wait("v", "vec", v_tz)
    for i in range(3):
        v_off = V(ve.tensor_copy(T.off4[:, i:32:4], T.tz[:, i:24:3]))
    filler()
    wait("v", "act", max(a_tab, a_vr))
    wait("v", "vec", v_off)
    v_sc = 0
    for t, s in enumerate(chain):
        x = _pos(t)
        win = T.tab[:, 0:C + CAP]
        off = T.off4[:, 4 * s:4 * s + 3]
        if t:
            wait("v", "vec", v_sc)
            late["pv"] = V(ve.tensor_copy(T.pv[:, x:x + CAP], win.indirect(off)))
            if t == 4:
                filler(len(todo))
                todo.extend((do_list, (PARTS[0], k)) for k in range(5))
            else:
                filler()
            wait("v", "vec", late["pv"])
        v_sc = V(ve.tensor_copy(win.indirect(off), T.vr[:, x:x + CAP]))
        if t:
            filler()
    filler(len(todo))
    wait("y", "vec", v_sc)
    for k in range(8):
        inc("dwrap", sy.dma_start(T.tw[16 * k:16 * k + 16, :], T.tab[16 * k:16 * k + 1, 0:C]), 16)
    inc("dfin", sy.dma_start(T.finq[:, C // 2:C].bitcast(u8), T.wc[:, 2 * C:4 * C]), 16)
    inc("dfin", sy.dma_start(T.fins[:, 0:C], T.ws[:]), 16)
    for k in range(5):
        do_list(PARTS[1], k)
    wait("s", "vec", late["pv"])
    a_h = A(sc.activation(T.hup[:, 16:16 + ALL], T.pv[:], Fn.Sign, bias=float(NONE - KEY // 8), scale=-1.0))

    def prod(ps, b, k, q, s, a, z, start, stop):
        return te.matmul_mx(T[ps][:, 512 * b:512 * b + z - a], T.eq[:, 128 * k:128 * k + 128],
                            T.es[:, 128 * k:128 * k + 128], T[q][:, a:z], T[s][:, a:z], start, stop)

    wait("t", "vec", max(late["w"], v_ep))
    wait("t", "act", late["ws"])
    for ps, a, z, _x, _y, _e in PARTS:
        for b in range(4):
            prod(ps, b, b, "wselq", "wsels", a, z, True, False)

    def arrived(stage):
        return sum(len(_engines(s, _stages(s)[stage], T, topo)[me])
                   for s in range(N) if s != me and me in _stages(s)[stage])

    stops = []
    for i, (ps, a, z, x, y, e) in enumerate(PARTS):
        w1, n = ZERO + z, (z - a) // 16
        wait("v", "arrec" if i == 0 else "arrlc", arrived(i))
        wait("s", "arres" if i == 0 else "arrls", arrived(i))
        wait("v", "vec", max(late["list", a], v_own, v_zq))
        wait("s", "vec", max(late["list", a], v_zq))
        wait("s", "act", a_own)
        for q, s, o, last in (("firq", "firs", x, False), ("secq", "secs", y, True)):
            vp = pickc(T[q], a, z, T.landq, 0, w1, T.fsl, o, o + n)
            ap = picks(T[s], a, z, T.lands, 0, w1, T.fsl, o, o + n)
            wait("t", "vec", max(vp, late["em"]))
            wait("t", "act", ap)
            for b in range(4):
                ins = prod(ps, b, 4 + b, q, s, a, z, False, last)
                if last:
                    stops.append(inc("ten", ins))

    wait("v", "dwrap", cnt["dwrap"])
    v_ti = V(ve.tensor_copy(T.ti[:], T.tw[:]))

    for i, (ps, a, z, _x, _y, _e) in enumerate(PARTS):
        vl = al = 0
        for b in range(4):
            out, src = T.h[:, 4 * a + b:4 * z:4], T[ps][:, 512 * b:512 * b + z - a]
            if b % 2 == 0:
                wait("v", "ten", stops[4 * i + b])
                vl = V(ve.tensor_copy(out, src))
                if i == 0 and b == 0:
                    wait("v", "vec", v_ti)
                    v_tf = V(ve.tensor_scalar(T.tf[:], T.ti[:], KEY - 1, None, Op.bitwise_and))
            else:
                wait("s", "ten", stops[4 * i + b])
                al = A(sc.activation(out, src, Fn.Copy))
        if i == 0:
            wait("v", "vec", v_tf)
            v_up = V(ve.tensor_scalar(T.upl[:], T.tf[:], float(NEW + ZERO - 16), float(NEW + ZERO - 16),
                                      Op.max, Op.subtract))
            v_fin = V(ve.tensor_copy(T.finl[:], T.tf[:]))
        wait("v", "vec", vl)
        wait("v", "act", al)
        x = NEW + ZERO
        v_q = V(ve.quantize_mx(T.finq[:, x + a:x + z], T.fins[:, x + a:x + z], T.h[:, 4 * a:4 * z]))

    wait("y", "vec", v_up)
    for k in range(8):
        c = 16 * (k // 2)
        inc("dup", sy.dma_start(T.upg[16 * k:16 * k + 16, :], T.upl[16 * k:16 * k + 16, c:c + 16]), 16)

    wait("v", "vec", max(v_q, v_fin))
    wait("v", "dfin", cnt["dfin"])
    wait("s", "vec", max(v_q, v_fin))
    wait("s", "dfin", cnt["dfin"])
    W = NEW + ZERO + ALL
    for j in range(4):
        vp = pickc(T.outq, 256 * j, 256 * j + 256, T.finq, 0, W, T.finl, 16 * j, 16 * j + 16)
        ap = picks(T.outs, 256 * j, 256 * j + 256, T.fins, 0, W, T.finl, 16 * j, 16 * j + 16)
        wait("y", "vec", vp)
        inc("dout", sy.dma_start(T.oc[:, 1024 * j:1024 * j + 1024], T.outq[:, 256 * j:256 * j + 256].bitcast(u8)), 16)
    wait("y", "act", ap)
    for k in range(4):
        inc("dout", sy.dma_start(T.osc[4 * k:4 * k + 4, :], T.outs[32 * k:32 * k + 4, :]), 16)
    wait("s", "dup", cnt["dup"])
    wait("s", "act", a_h)
    a_up = A(sc.activation(T.upr[:], T.hup[:].indirect(T.upg[:]), Fn.Identity, bias=1.5, scale=0.5))
    wait("s", "act", a_up)
    for k in range(4):
        inc("dout", sc.dma_start(T.up[:, 256 * k:256 * k + 256], T.upr[32 * k:32 * k + 1, :]), 16)

    wait("g", "sent", sent)
    for name in ("vec", "act", "ten", "gpc", "dout"):
        wait("g", name, cnt[name])
